import numpy as np
import ml_dtypes


def mxq(x, axis, fmt="e4m3"):
    dtype, down = {"e4m3": (ml_dtypes.float8_e4m3fn, 7), "e5m2": (ml_dtypes.float8_e5m2, 14)}[fmt]
    v = np.moveaxis(np.asarray(x, np.float32).astype(ml_dtypes.bfloat16).astype(np.float64), axis, -1)
    blocks = v.reshape(v.shape[:-1] + (-1, 32))
    amax = np.abs(blocks).max(-1, keepdims=True)
    byte = np.maximum(np.where(amax > 0, np.frexp(amax)[1] - 1 + 127, 0) - down, 1)
    scale = np.exp2(byte - 127.0)
    codes = (blocks / scale).astype(np.float32).astype(dtype).astype(np.float64)
    return np.moveaxis((codes * scale).reshape(v.shape), -1, axis)


WIDE = False


def mx_kscale(k):
    if not WIDE:
        return np.ones(k)
    levels = np.array([30, -30])
    if k % 512:
        return np.exp2(np.random.permutation(np.resize(levels, k // 32))).repeat(32)
    a = np.empty((k // 512, 16))
    for p in range(k // 512):
        a[p, :8] = np.random.permutation(np.resize(levels, 8))
        for g in range(8):
            far = levels[np.abs(levels - a[p, g]) >= 10]
            a[p, g + 8] = far[np.random.randint(len(far))]
    return np.exp2(a.ravel()).repeat(32)


def f64(x):
    return np.asarray(x).astype(np.float64)


def striped(idx):
    return np.tile(np.asarray(idx).reshape(-1, 16).T, (8, 1)).astype(np.uint16)


def unstriped(offs):
    return offs[:16].T.reshape(-1).astype(np.int64)


def striped8(idx):
    return np.asarray(idx).reshape(8, -1, 16).transpose(0, 2, 1).reshape(128, -1).astype(np.uint16)


def unstriped8(offs):
    return offs.reshape(8, 16, -1).transpose(0, 2, 1).reshape(8, -1).astype(np.int64)


def pick8(x, idx, run):
    r = np.arange(len(x))
    return x[r[:, None], idx[r % (8 * run) // run]]


E2M1 = np.array([0.0, 0.5, 1.0, 1.5, 2.0, 3.0, 4.0, 6.0, -0.0, -0.5, -1.0, -1.5, -2.0, -3.0, -4.0, -6.0])


def pack_weight(w, fmt):
    k, n = w.shape
    w = f64(np.asarray(w, np.float32).astype(ml_dtypes.bfloat16)).reshape(k // 32, 32, n)
    amax = np.abs(w).max(1)
    if fmt in ("e4m3", "e5m2"):
        byte = np.frexp(amax)[1] - 1 + 127 - (7 if fmt == "e4m3" else 14)
    else:
        mant, ex = np.frexp(amax / 6.0)
        byte = np.where(mant > 0.5, ex, ex - 1) + 127
    byte = np.clip(np.where(amax > 0, byte, 1), 1, 254)
    scaled = (w * np.exp2(127.0 - byte)[:, None, :]).reshape(k, n).astype(np.float32)
    by_word = np.ascontiguousarray(scaled.reshape(k // 512, 128, 4, n).transpose(0, 1, 3, 2))
    if fmt in ("e4m3", "e5m2"):
        words = by_word.astype(ml_dtypes.float8_e4m3fn if fmt == "e4m3" else ml_dtypes.float8_e5m2).view(np.uint8)
    else:
        c = by_word.astype(ml_dtypes.float4_e2m1fn).view(np.uint8) & 0xF
        words = (c[..., 0::2] | (c[..., 1::2] << 4)).reshape(k // 512, 128, 2 * n)
    return np.ascontiguousarray(words), np.ascontiguousarray(byte.astype(np.uint8).reshape(k // 512, 16, n))


def unpack_weight(words, scales, fmt):
    g, _, n = scales.shape
    words = np.ascontiguousarray(words).reshape(g, 128, n, -1)
    if fmt in ("e4m3", "e5m2"):
        vals = words.view(ml_dtypes.float8_e4m3fn if fmt == "e4m3" else ml_dtypes.float8_e5m2).astype(np.float64)
    else:
        nib = np.empty((g, 128, n, 4), np.uint8)
        nib[..., 0::2] = words & 0xF
        nib[..., 1::2] = words >> 4
        vals = E2M1[nib]
    vals = vals * np.repeat(np.exp2(scales.astype(np.float64) - 127.0), 8, axis=1)[..., None]
    return vals.transpose(0, 1, 3, 2).reshape(g * 512, n)


K, T, J, R, V, C, O, N, E = 512, 1024, 256, 512, 1024, 512, 256, 256, 512


def setup_inputs():
    n = np.random.standard_normal
    idx = np.random.permutation(V)[:R]
    idx2 = np.random.permutation(T)[:J]
    idx3 = np.stack([np.random.permutation(C)[:J] for _ in range(8)])
    idx4 = np.stack([np.random.permutation(C)[:O] for _ in range(8)])
    idx5 = np.random.permutation(E)[:O]
    fk = mx_kscale(K)
    fr = mx_kscale(R)
    xtp = pack_weight(n((K, T)) / fk[:, None], "e2m1")
    wtp = pack_weight(n((K, V)) * 1 / np.sqrt(K) * fk[:, None], "e5m2")
    wbp = pack_weight(n((R, N)) * 1 / np.sqrt(R) / fr[:, None], "e4m3")
    return {
        "xt_words": xtp[0],
        "xt_scales": xtp[1],
        "wt_words": wtp[0],
        "wt_scales": wtp[1],
        "sa": (np.random.uniform(0.5, 1.6, (R, 1)) * fr[:, None]).astype(np.float32),
        "wb_words": wbp[0],
        "wb_scales": wbp[1],
        "so": (np.random.uniform(0.5, 1.6, (N, 1))).astype(np.float32),
        "offs": striped(idx),
        "offs2": striped(idx2),
        "offs3": striped8(idx3),
        "offs4": striped8(idx4),
        "offs5": striped(idx5),
    }


def reference(xt_words, xt_scales, wt_words, wt_scales, sa, wb_words, wb_scales, so, offs, offs2, offs3, offs4, offs5):
    idx = unstriped(offs)
    idx2 = unstriped(offs2)
    idx3 = unstriped8(offs3)
    idx4 = unstriped8(offs4)
    idx5 = unstriped(offs5)
    xtu = unpack_weight(xt_words, xt_scales, "e2m1")
    wtu = unpack_weight(wt_words, wt_scales, "e5m2")
    wbu = unpack_weight(wb_words, wb_scales, "e4m3")
    wtidxg = wtu[:, idx]
    xtidx2g = xtu[:, idx2]
    a = wtidxg.T @ xtidx2g
    pw = np.zeros((R, C))
    pw[np.arange(R)[:, None], idx3[np.arange(R) % 512 // 64]] = a * f64(sa)
    hid = pick8(pw, idx4, 64)
    hidq = mxq(hid, 0, "e5m2")
    p = wbu.T @ hidq
    y = np.zeros((N, E))
    y[:, idx5] = p * f64(so)
    return y

@@ -1,0 +1,125 @@
+from contextlib import ExitStack
+
+import concourse.mybir as mybir
+
+K, T, J, R, V, C, O, N, E = 512, 1024, 256, 512, 1024, 512, 256, 256, 512
+FLOPS = 2 * K * R * J + 2 * R * N * O
+
+F32 = mybir.dt.float32
+BF16 = mybir.dt.bfloat16
+I32 = mybir.dt.int32
+U32 = mybir.dt.uint32
+U16 = mybir.dt.uint16
+U8 = mybir.dt.uint8
+E4M3 = mybir.dt.float8_e4m3fn_x4
+E5M2 = mybir.dt.float8_e5m2_x4
+E2M1 = mybir.dt.float4_e2m1fn_x4
+COPY = mybir.ActivationFunctionType.Copy
+
+P = 128
+PACK = 4
+HALF = O // 2
+
+
+def load_scale_rows(queue, plane, scales):
+    for quad in range(4):
+        queue.dma_start(
+            plane[32 * quad : 32 * quad + 4, :].bitcast(I32),
+            scales[0, 4 * quad : 4 * quad + 4, :].bitcast(I32),
+        )
+
+
+def tile_list_ownstep_kernel(tc, xt_words, xt_scales, wt_words, wt_scales, sa, wb_words, wb_scales, so, offs, offs2, offs3, offs4, offs5, out):
+    nc = tc.nc
+    with ExitStack() as ctx:
+        keep = ctx.enter_context(tc.tile_pool(name="keep", bufs=1))
+        psum = ctx.enter_context(tc.psum_pool(name="psum", bufs=1))
+
+        l1 = keep.tile([P, R // 16], U16, name="l1")
+        l2 = keep.tile([P, J // 16], U16, name="l2")
+        l3 = keep.tile([P, J // 16], U16, name="l3")
+        l4 = keep.tile([P, O // 16], U16, name="l4")
+        l5 = keep.tile([P, O // 16], U16, name="l5")
+        wt_w = keep.tile([P, V], U32, name="wt_w", align_bytes=64)
+        wt_s = keep.tile([P, V], U8, name="wt_s", align_bytes=64)
+        xt_w = keep.tile([P, T], U16, name="xt_w", align_bytes=64)
+        xt_s = keep.tile([P, T], U8, name="xt_s", align_bytes=64)
+        wb_w = keep.tile([P, N], U32, name="wb_w", align_bytes=64)
+        wb_s = keep.tile([P, N], U8, name="wb_s", align_bytes=64)
+        sa_t = keep.tile([P, PACK], F32, name="sa_t")
+        so_t = keep.tile([P, N // P], F32, name="so_t")
+
+        nc.vector.memset(wt_s[:].bitcast(I32), 0)
+        nc.vector.memset(xt_s[:].bitcast(I32), 0)
+        nc.gpsimd.memset(wb_s[:].bitcast(I32), 0)
+
+        nc.sync.dma_start(l2[:], offs2)
+        nc.sync.dma_start(xt_w[:].bitcast(I32), xt_words[0].bitcast(I32))
+        nc.sync.dma_start(l1[:], offs)
+        load_scale_rows(nc.sync, wt_s, wt_scales)
+        nc.sync.dma_start(wt_w[:].bitcast(I32), wt_words[0].rearrange("p n t -> p (n t)").bitcast(I32))
+        nc.sync.dma_start(l3[:], offs3)
+        nc.sync.dma_start(sa_t[:], sa.rearrange("(p t) o -> p (t o)", t=PACK))
+        load_scale_rows(nc.sync, xt_s, xt_scales)
+        nc.sync.dma_start(l4[:], offs4)
+        nc.sync.dma_start(wb_w[:].bitcast(I32), wb_words[0].rearrange("p n t -> p (n t)").bitcast(I32))
+        load_scale_rows(nc.sync, wb_s, wb_scales)
+        nc.sync.dma_start(l5[:], offs5)
+        with nc.allow_non_contiguous_dma(reason="one weight a partition and output tile"):
+            nc.sync.dma_start(so_t[:], so.rearrange("(m p) o -> p (m o)", p=P))
+
+        boards = [keep.tile([P, C], F32, name="board%d" % t) for t in range(PACK)]
+        for t in range(PACK):
+            nc.vector.memset(boards[t][:], 0.0)
+
+        wg_w = keep.tile([P, R], U32, name="wg_w", align_bytes=64)
+        wg_s = keep.tile([P, R], U8, name="wg_s", align_bytes=64)
+        xg_w = keep.tile([P, J], U16, name="xg_w", align_bytes=64)
+        xg_s = [keep.tile([P, HALF], U8, name="xg_s%d" % h, align_bytes=64) for h in range(2)]
+        lcols = HALF // 16
+        nc.vector.tensor_copy(xg_w[:], xt_w[:].indirect(l2[:]))
+        nc.vector.tensor_copy(wg_s[:].rearrange("p (t q) -> p q t", t=PACK), wt_s[:].indirect(l1[:]))
+        nc.vector.tensor_copy(wg_w[:].rearrange("p (t q) -> p q t", t=PACK), wt_w[:].indirect(l1[:]))
+        for h in range(2):
+            nc.vector.tensor_copy(xg_s[h][:], xt_s[:].indirect(l2[:, h * lcols : (h + 1) * lcols]))
+
+        for pair in range(2):
+            for h in range(2):
+                for t in (2 * pair, 2 * pair + 1):
+                    cols = slice(t * P, (t + 1) * P)
+                    a_ps = psum.tile([P, HALF], F32, name="a_ps%d%d" % (t, h), tag="bank%d" % (2 * t + h))
+                    nc.tensor.matmul_mx(
+                        out=a_ps[:], lhsT=wg_w[:, cols].bitcast(E5M2), lhsT_scale=wg_s[:, cols],
+                        rhs=xg_w[:, h * HALF : (h + 1) * HALF].bitcast(E2M1), rhs_scale=xg_s[h][:], start=True, stop=True,
+                    )
+                    a_sb = keep.tile([P, HALF], F32, name="a_sb%d%d" % (t, h), tag="rows%d" % (2 * h + t if pair == 0 else 4 + 2 * h + t))
+                    nc.vector.tensor_copy(a_sb[:], a_ps[:])
+                    nc.scalar.activation(boards[t][:].indirect(l3[:, h * lcols : (h + 1) * lcols]), a_sb[:], COPY, scale=sa_t[:, t : t + 1])
+
+        pages = [keep.tile([P, E], F32, name="page%d" % m, tag="rows%d" % m) for m in range(N // P)]
+        for m in range(N // P):
+            nc.vector.memset(pages[m][:], 0.0)
+
+        p_sb = {}
+        for h in range(2):
+            hid = keep.tile([P, PACK * HALF], BF16, name="hid%d" % h, align_bytes=64)
+            for t in range(PACK):
+                nc.scalar.activation(hid[:, t : PACK * HALF : PACK], boards[t][:].indirect(l4[:, h * lcols : (h + 1) * lcols]), COPY)
+            hq_w = keep.tile([P, HALF], U32, name="hq_w%d" % h, align_bytes=64)
+            hq_s = keep.tile([P, HALF], U8, name="hq_s%d" % h, align_bytes=64)
+            nc.vector.quantize_mx(out=hq_w[:].bitcast(E5M2), scales=hq_s[:], in_=hid[:])
+            for m in range(N // P):
+                cols = slice(m * P, (m + 1) * P)
+                p_ps = psum.tile([P, HALF], F32, name="p_ps%d%d" % (h, m), tag="bank%d" % (2 * h + m))
+                nc.tensor.matmul_mx(
+                    out=p_ps[:], lhsT=wb_w[:, cols].bitcast(E4M3), lhsT_scale=wb_s[:, cols],
+                    rhs=hq_w[:].bitcast(E5M2), rhs_scale=hq_s[:], start=True, stop=True,
+                )
+                p_sb[h, m] = keep.tile([P, HALF], F32, name="p_sb%d%d" % (h, m))
+                nc.vector.tensor_copy(p_sb[h, m][:], p_ps[:])
+
+        for h in range(2):
+            for m in range(N // P):
+                nc.scalar.activation(pages[m][:].indirect(l5[:, h * lcols : (h + 1) * lcols]), p_sb[h, m][:], COPY, scale=so_t[:, m : m + 1])
+        for m in range(N // P):
+            nc.sync.dma_start(out[m * P : (m + 1) * P, :], pages[m][:])

@@ -49,18 +49,20 @@ def tile_list_ownstep_kernel(tc, xt_words, xt_scales, wt_words, wt_scales, sa, w
         sa_t = keep.tile([P, PACK], F32, name="sa_t")
         so_t = keep.tile([P, N // P], F32, name="so_t")
 
-        nc.vector.memset(wt_s[:].bitcast(I32), 0)
         nc.vector.memset(xt_s[:].bitcast(I32), 0)
         nc.gpsimd.memset(wb_s[:].bitcast(I32), 0)
 
-        nc.sync.dma_start(l2[:], offs2)
-        nc.sync.dma_start(xt_w[:].bitcast(I32), xt_words[0].bitcast(I32))
+        for quad in range(4):
+            rows = wt_scales[0, 4 * quad : 4 * quad + 4, :].bitcast(I32).rearrange("r c -> (r c)")
+            queue = nc.sync if quad < 2 else nc.scalar
+            queue.dma_start(wt_s[32 * quad : 32 * quad + 32, :].bitcast(I32), rows.partition_broadcast(8))
         nc.sync.dma_start(l1[:], offs)
-        load_scale_rows(nc.sync, wt_s, wt_scales)
         nc.sync.dma_start(wt_w[:].bitcast(I32), wt_words[0].rearrange("p n t -> p (n t)").bitcast(I32))
+        nc.sync.dma_start(xt_w[:].bitcast(I32), xt_words[0].bitcast(I32))
+        nc.sync.dma_start(l2[:], offs2)
+        load_scale_rows(nc.sync, xt_s, xt_scales)
         nc.sync.dma_start(l3[:], offs3)
         nc.sync.dma_start(sa_t[:], sa.rearrange("(p t) o -> p (t o)", t=PACK))
-        load_scale_rows(nc.sync, xt_s, xt_scales)
         nc.sync.dma_start(l4[:], offs4)
         nc.sync.dma_start(wb_w[:].bitcast(I32), wb_words[0].rearrange("p n t -> p (n t)").bitcast(I32))
         load_scale_rows(nc.sync, wb_s, wb_scales)
@@ -70,42 +72,56 @@ def tile_list_ownstep_kernel(tc, xt_words, xt_scales, wt_words, wt_scales, sa, w
 
         boards = [keep.tile([P, C], F32, name="board%d" % t) for t in range(PACK)]
         for t in range(PACK):
-            nc.vector.memset(boards[t][:], 0.0)
+            (nc.vector if t < PACK - 1 else nc.gpsimd).memset(boards[t][:], 0.0)
 
         wg_w = keep.tile([P, R], U32, name="wg_w", align_bytes=64)
         wg_s = keep.tile([P, R], U8, name="wg_s", align_bytes=64)
-        xg_w = keep.tile([P, J], U16, name="xg_w", align_bytes=64)
-        xg_s = [keep.tile([P, HALF], U8, name="xg_s%d" % h, align_bytes=64) for h in range(2)]
         lcols = HALF // 16
-        nc.vector.tensor_copy(xg_w[:], xt_w[:].indirect(l2[:]))
+
+        def gather_tokens(h):
+            words = keep.tile([P, HALF], U16, name="xg_w%d" % h, tag="xg_w", align_bytes=64)
+            scales = keep.tile([P, HALF], U8, name="xg_s%d" % h, tag="xg_s", align_bytes=64)
+            return words, scales, l2[:, h * lcols : (h + 1) * lcols]
+
+        xg = [gather_tokens(0)]
         nc.vector.tensor_copy(wg_s[:].rearrange("p (t q) -> p q t", t=PACK), wt_s[:].indirect(l1[:]))
         nc.vector.tensor_copy(wg_w[:].rearrange("p (t q) -> p q t", t=PACK), wt_w[:].indirect(l1[:]))
-        for h in range(2):
-            nc.vector.tensor_copy(xg_s[h][:], xt_s[:].indirect(l2[:, h * lcols : (h + 1) * lcols]))
+        nc.vector.tensor_copy(xg[0][0][:], xt_w[:].indirect(xg[0][2]))
+        nc.vector.tensor_copy(xg[0][1][:], xt_s[:].indirect(xg[0][2]))
 
-        for pair in range(2):
-            for h in range(2):
-                for t in (2 * pair, 2 * pair + 1):
-                    cols = slice(t * P, (t + 1) * P)
-                    a_ps = psum.tile([P, HALF], F32, name="a_ps%d%d" % (t, h), tag="bank%d" % (2 * t + h))
-                    nc.tensor.matmul_mx(
-                        out=a_ps[:], lhsT=wg_w[:, cols].bitcast(E5M2), lhsT_scale=wg_s[:, cols],
-                        rhs=xg_w[:, h * HALF : (h + 1) * HALF].bitcast(E2M1), rhs_scale=xg_s[h][:], start=True, stop=True,
-                    )
-                    a_sb = keep.tile([P, HALF], F32, name="a_sb%d%d" % (t, h), tag="rows%d" % (2 * h + t if pair == 0 else 4 + 2 * h + t))
-                    nc.vector.tensor_copy(a_sb[:], a_ps[:])
-                    nc.scalar.activation(boards[t][:].indirect(l3[:, h * lcols : (h + 1) * lcols]), a_sb[:], COPY, scale=sa_t[:, t : t + 1])
+        def first_stage(t, j0, width, evacuate, tag):
+            cols = slice(t * P, (t + 1) * P)
+            a_ps = psum.tile([P, width], F32, name="a_ps%d_%d" % (t, j0), tag="bank%d" % tag)
+            nc.tensor.matmul_mx(
+                out=a_ps[:], lhsT=wg_w[:, cols].bitcast(E5M2), lhsT_scale=wg_s[:, cols],
+                rhs=xg[j0 // HALF][0][:].bitcast(E2M1), rhs_scale=xg[j0 // HALF][1][:], start=True, stop=True,
+            )
+            a_sb = keep.tile([P, width], F32, name="a_sb%d_%d" % (t, j0), tag="rows%d" % tag, align_bytes=64)
+            evacuate(a_sb[:], a_ps[:])
+            return a_sb
 
-        pages = [keep.tile([P, E], F32, name="page%d" % m, tag="rows%d" % m) for m in range(N // P)]
+        def put_rows(t, j0, width, a_sb):
+            nc.scalar.activation(boards[t][:].indirect(l3[:, j0 // 16 : (j0 + width) // 16]), a_sb[:], COPY, scale=sa_t[:, t : t + 1])
+
+        first = [first_stage(t, 0, HALF, nc.scalar.copy if t == 1 else nc.vector.tensor_copy, t) for t in range(PACK)]
+        for t in range(PACK):
+            put_rows(t, 0, HALF, first[t])
+        xg.append(gather_tokens(1))
+        nc.vector.tensor_copy(xg[1][0][:], xt_w[:].indirect(xg[1][2]))
+        nc.vector.tensor_copy(xg[1][1][:], xt_s[:].indirect(xg[1][2]))
+        for t in range(PACK):
+            put_rows(t, HALF, HALF, first_stage(t, HALF, HALF, nc.vector.tensor_copy, PACK + t))
+
+        pages = [keep.tile([P, E], F32, name="page%d" % m, tag="rows%d" % m, align_bytes=64) for m in range(N // P)]
         for m in range(N // P):
             nc.vector.memset(pages[m][:], 0.0)
 
         p_sb = {}
         for h in range(2):
-            hid = keep.tile([P, PACK * HALF], BF16, name="hid%d" % h, align_bytes=64)
+            hid = keep.tile([P, PACK * HALF], BF16, name="hid%d" % h, tag=("hid0", "rows7")[h], align_bytes=64)
             for t in range(PACK):
                 nc.scalar.activation(hid[:, t : PACK * HALF : PACK], boards[t][:].indirect(l4[:, h * lcols : (h + 1) * lcols]), COPY)
-            hq_w = keep.tile([P, HALF], U32, name="hq_w%d" % h, align_bytes=64)
+            hq_w = keep.tile([P, HALF], U32, name="hq_w%d" % h, tag="hq_w", align_bytes=64)
             hq_s = keep.tile([P, HALF], U8, name="hq_s%d" % h, align_bytes=64)
             nc.vector.quantize_mx(out=hq_w[:].bitcast(E5M2), scales=hq_s[:], in_=hid[:])
             for m in range(N // P):

from contextlib import ExitStack

import concourse.mybir as mybir

K, T, J, R, V, C, O, N, E = 512, 1024, 256, 512, 1024, 512, 256, 256, 512
FLOPS = 2 * K * R * J + 2 * R * N * O

F32 = mybir.dt.float32
BF16 = mybir.dt.bfloat16
I32 = mybir.dt.int32
U32 = mybir.dt.uint32
U16 = mybir.dt.uint16
U8 = mybir.dt.uint8
E4M3 = mybir.dt.float8_e4m3fn_x4
E5M2 = mybir.dt.float8_e5m2_x4
E2M1 = mybir.dt.float4_e2m1fn_x4
COPY = mybir.ActivationFunctionType.Copy

P = 128
PACK = 4
HALF = O // 2


def load_scale_rows(queue, plane, scales):
    for quad in range(4):
        queue.dma_start(
            plane[32 * quad : 32 * quad + 4, :].bitcast(I32),
            scales[0, 4 * quad : 4 * quad + 4, :].bitcast(I32),
        )


def tile_list_ownstep_kernel(tc, xt_words, xt_scales, wt_words, wt_scales, sa, wb_words, wb_scales, so, offs, offs2, offs3, offs4, offs5, out):
    nc = tc.nc
    with ExitStack() as ctx:
        keep = ctx.enter_context(tc.tile_pool(name="keep", bufs=1))
        psum = ctx.enter_context(tc.psum_pool(name="psum", bufs=1))

        l1 = keep.tile([P, R // 16], U16, name="l1")
        l2 = keep.tile([P, J // 16], U16, name="l2")
        l3 = keep.tile([P, J // 16], U16, name="l3")
        l4 = keep.tile([P, O // 16], U16, name="l4")
        l5 = keep.tile([P, O // 16], U16, name="l5")
        wt_w = keep.tile([P, V], U32, name="wt_w", align_bytes=64)
        wt_s = keep.tile([P, V], U8, name="wt_s", align_bytes=64)
        xt_w = keep.tile([P, T], U16, name="xt_w", align_bytes=64)
        xt_s = keep.tile([P, T], U8, name="xt_s", align_bytes=64)
        wb_w = keep.tile([P, N], U32, name="wb_w", align_bytes=64)
        wb_s = keep.tile([P, N], U8, name="wb_s", align_bytes=64)
        sa_t = keep.tile([P, PACK], F32, name="sa_t")
        so_t = keep.tile([P, N // P], F32, name="so_t")

        nc.vector.memset(xt_s[:].bitcast(I32), 0)
        nc.gpsimd.memset(wb_s[:].bitcast(I32), 0)

        for quad in range(4):
            rows = wt_scales[0, 4 * quad : 4 * quad + 4, :].bitcast(I32).rearrange("r c -> (r c)")
            queue = nc.sync if quad < 2 else nc.scalar
            queue.dma_start(wt_s[32 * quad : 32 * quad + 32, :].bitcast(I32), rows.partition_broadcast(8))
        nc.sync.dma_start(l1[:], offs)
        nc.sync.dma_start(wt_w[:].bitcast(I32), wt_words[0].rearrange("p n t -> p (n t)").bitcast(I32))
        nc.sync.dma_start(xt_w[:].bitcast(I32), xt_words[0].bitcast(I32))
        nc.sync.dma_start(l2[:], offs2)
        load_scale_rows(nc.sync, xt_s, xt_scales)
        nc.sync.dma_start(l3[:], offs3)
        nc.sync.dma_start(sa_t[:], sa.rearrange("(p t) o -> p (t o)", t=PACK))
        nc.sync.dma_start(l4[:], offs4)
        nc.sync.dma_start(wb_w[:].bitcast(I32), wb_words[0].rearrange("p n t -> p (n t)").bitcast(I32))
        load_scale_rows(nc.sync, wb_s, wb_scales)
        nc.sync.dma_start(l5[:], offs5)
        with nc.allow_non_contiguous_dma(reason="one weight a partition and output tile"):
            nc.sync.dma_start(so_t[:], so.rearrange("(m p) o -> p (m o)", p=P))

        boards = [keep.tile([P, C], F32, name="board%d" % t) for t in range(PACK)]
        for t in range(PACK):
            (nc.vector if t < PACK - 1 else nc.gpsimd).memset(boards[t][:], 0.0)

        wg_w = keep.tile([P, R], U32, name="wg_w", align_bytes=64)
        wg_s = keep.tile([P, R], U8, name="wg_s", align_bytes=64)
        lcols = HALF // 16

        def gather_tokens(h):
            words = keep.tile([P, HALF], U16, name="xg_w%d" % h, tag="xg_w", align_bytes=64)
            scales = keep.tile([P, HALF], U8, name="xg_s%d" % h, tag="xg_s", align_bytes=64)
            return words, scales, l2[:, h * lcols : (h + 1) * lcols]

        xg = [gather_tokens(0)]
        nc.vector.tensor_copy(wg_s[:].rearrange("p (t q) -> p q t", t=PACK), wt_s[:].indirect(l1[:]))
        nc.vector.tensor_copy(wg_w[:].rearrange("p (t q) -> p q t", t=PACK), wt_w[:].indirect(l1[:]))
        nc.vector.tensor_copy(xg[0][0][:], xt_w[:].indirect(xg[0][2]))
        nc.vector.tensor_copy(xg[0][1][:], xt_s[:].indirect(xg[0][2]))

        def first_stage(t, j0, width, evacuate, tag):
            cols = slice(t * P, (t + 1) * P)
            a_ps = psum.tile([P, width], F32, name="a_ps%d_%d" % (t, j0), tag="bank%d" % tag)
            nc.tensor.matmul_mx(
                out=a_ps[:], lhsT=wg_w[:, cols].bitcast(E5M2), lhsT_scale=wg_s[:, cols],
                rhs=xg[j0 // HALF][0][:].bitcast(E2M1), rhs_scale=xg[j0 // HALF][1][:], start=True, stop=True,
            )
            a_sb = keep.tile([P, width], F32, name="a_sb%d_%d" % (t, j0), tag="rows%d" % tag, align_bytes=64)
            evacuate(a_sb[:], a_ps[:])
            return a_sb

        def put_rows(t, j0, width, a_sb):
            nc.scalar.activation(boards[t][:].indirect(l3[:, j0 // 16 : (j0 + width) // 16]), a_sb[:], COPY, scale=sa_t[:, t : t + 1])

        first = [first_stage(t, 0, HALF, nc.scalar.copy if t == 1 else nc.vector.tensor_copy, t) for t in range(PACK)]
        for t in range(PACK):
            put_rows(t, 0, HALF, first[t])
        xg.append(gather_tokens(1))
        nc.vector.tensor_copy(xg[1][0][:], xt_w[:].indirect(xg[1][2]))
        nc.vector.tensor_copy(xg[1][1][:], xt_s[:].indirect(xg[1][2]))
        for t in range(PACK):
            put_rows(t, HALF, HALF, first_stage(t, HALF, HALF, nc.vector.tensor_copy, PACK + t))

        pages = [keep.tile([P, E], F32, name="page%d" % m, tag="rows%d" % m, align_bytes=64) for m in range(N // P)]
        for m in range(N // P):
            nc.vector.memset(pages[m][:], 0.0)

        p_sb = {}
        for h in range(2):
            hid = keep.tile([P, PACK * HALF], BF16, name="hid%d" % h, tag=("hid0", "rows7")[h], align_bytes=64)
            for t in range(PACK):
                nc.scalar.activation(hid[:, t : PACK * HALF : PACK], boards[t][:].indirect(l4[:, h * lcols : (h + 1) * lcols]), COPY)
            hq_w = keep.tile([P, HALF], U32, name="hq_w%d" % h, tag="hq_w", align_bytes=64)
            hq_s = keep.tile([P, HALF], U8, name="hq_s%d" % h, align_bytes=64)
            nc.vector.quantize_mx(out=hq_w[:].bitcast(E5M2), scales=hq_s[:], in_=hid[:])
            for m in range(N // P):
                cols = slice(m * P, (m + 1) * P)
                p_ps = psum.tile([P, HALF], F32, name="p_ps%d%d" % (h, m), tag="bank%d" % (2 * h + m))
                nc.tensor.matmul_mx(
                    out=p_ps[:], lhsT=wb_w[:, cols].bitcast(E4M3), lhsT_scale=wb_s[:, cols],
                    rhs=hq_w[:].bitcast(E5M2), rhs_scale=hq_s[:], start=True, stop=True,
                )
                p_sb[h, m] = keep.tile([P, HALF], F32, name="p_sb%d%d" % (h, m))
                nc.vector.tensor_copy(p_sb[h, m][:], p_ps[:])

        for h in range(2):
            for m in range(N // P):
                nc.scalar.activation(pages[m][:].indirect(l5[:, h * lcols : (h + 1) * lcols]), p_sb[h, m][:], COPY, scale=so_t[:, m : m + 1])
        for m in range(N // P):
            nc.sync.dma_start(out[m * P : (m + 1) * P, :], pages[m][:])
